import numpy as np
import ml_dtypes


def mxq(x, axis, fmt="e4m3"):
    dtype, down = {"e4m3": (ml_dtypes.float8_e4m3fn, 7), "e5m2": (ml_dtypes.float8_e5m2, 14)}[fmt]
    v = np.moveaxis(np.asarray(x, np.float32).astype(ml_dtypes.bfloat16).astype(np.float64), axis, -1)
    blocks = v.reshape(v.shape[:-1] + (-1, 32))
    amax = np.abs(blocks).max(-1, keepdims=True)
    byte = np.maximum(np.where(amax > 0, np.frexp(amax)[1] - 1 + 127, 0) - down, 1)
    scale = np.exp2(byte - 127.0)
    codes = (blocks / scale).astype(np.float32).astype(dtype).astype(np.float64)
    return np.moveaxis((codes * scale).reshape(v.shape), -1, axis)


WIDE = False


def mx_kscale(k):
    if not WIDE:
        return np.ones(k)
    levels = np.array([24, -24, 12, -12, 0])
    if k % 512:
        return np.exp2(np.random.permutation(np.resize(levels, k // 32))).repeat(32)
    a = np.empty((k // 512, 16))
    for p in range(k // 512):
        a[p, :8] = np.random.permutation(np.resize(levels, 8))
        for g in range(8):
            far = levels[np.abs(levels - a[p, g]) >= 10]
            a[p, g + 8] = far[np.random.randint(len(far))]
    return np.exp2(a.ravel()).repeat(32)


def f64(x):
    return np.asarray(x).astype(np.float64)


def striped8(idx):
    return np.concatenate([v.reshape(-1, 16).T for v in idx]).astype(np.uint16)


def unstriped8(offs):
    return np.stack([offs[16 * g:16 * g + 16].T.reshape(-1) for g in range(8)]).astype(np.int64)


def split(x):
    m, e = np.frexp(f64(x))
    hi = np.ldexp(np.trunc(16.0 * m) / 16.0, e)
    return hi, f64(x) - hi


def sigm(f):
    return 1.0 / (1.0 + np.exp(-np.maximum(f, -700.0)))


K, N, T, J = 1024, 512, 2048, 1024


def setup_inputs():
    n = np.random.standard_normal
    s = mx_kscale(K)[:, None]
    return {
        "xT": (n((K, T)) * s).astype(np.float32),
        "wgt": np.repeat(np.random.uniform(0.5, 2.0, (8, J)), 16, axis=0).astype(np.float32),
        "wk": (n((K, N)) / np.sqrt(K) / s).astype(np.float32),
        "wv": (n((K, N)) / np.sqrt(K) / s).astype(np.float32),
        "bg": (0.3 * n(N) - 1.0).astype(np.float32),
        "res": (n((N, J))).astype(np.float32),
        "offs": striped8(np.stack([np.random.permutation(T)[:J] for _ in range(8)])),
    }


def reference(xT, wgt, wk, wv, bg, res, offs):
    idx = unstriped8(offs)
    rows = np.arange(K)
    xg = f64(wgt)[rows // 4 % 128] * f64(xT)[rows[:, None], idx[rows % 512 // 64]]
    xT_ = mxq(xg, 0, "e4m3")
    wk_hi, wk_lo = split(wk)
    wk_hi_, wk_lo_ = mxq(wk_hi, 0, "e4m3"), mxq(wk_lo, 0, "e4m3")
    wv_ = mxq(f64(wv), 0, "e4m3")
    ke = wk_hi_.T @ xT_ + wk_lo_.T @ xT_
    ve = wv_.T @ xT_
    gate = sigm(ke + f64(bg)[:, None])
    return f64(res) + gate * (ve - f64(res))

@@ -1,0 +1,229 @@
+from contextlib import ExitStack
+
+import concourse.mybir as mybir
+
+K, N, T, J = 1024, 512, 2048, 1024
+FLOPS = 3 * 2 * K * N * J
+
+F32 = mybir.dt.float32
+BF16 = mybir.dt.bfloat16
+I32 = mybir.dt.int32
+U32 = mybir.dt.uint32
+U16 = mybir.dt.uint16
+U8 = mybir.dt.uint8
+FP8X4 = mybir.dt.float8_e4m3fn_x4
+ALU = mybir.AluOpType
+ACT = mybir.ActivationFunctionType
+
+P = 128
+PACK = 4
+K_PASS = P * PACK
+PASSES = K // K_PASS
+HALF = 512
+HALVES = J // HALF
+N_TILES = N // P
+LIST_COLS = HALF // 16
+HI_MASK_PAIR = 0xFFF0FFF0 - (1 << 32)
+
+
+def tile_list_hl_hway_kernel(tc, xT, wgt, wk, wv, bg, res, offs, out):
+    nc = tc.nc
+    with ExitStack() as ctx:
+        keep = ctx.enter_context(tc.tile_pool(name="keep", bufs=1))
+        ring = ctx.enter_context(tc.tile_pool(name="ring", bufs=3))
+        gates = ctx.enter_context(tc.tile_pool(name="gates", bufs=4))
+        psum = ctx.enter_context(tc.psum_pool(name="psum", bufs=1))
+
+        offs_sb = keep.tile([P, J // 16], U16, name="offs_sb")
+        wgt_sb = keep.tile([P, J], F32, name="wgt_sb")
+        bg_sb = keep.tile([P, N_TILES], F32, name="bg_sb")
+        planes = {(a, i): keep.tile([P, T], F32, name="plane%d%d" % (a, i)) for a in range(PASSES) for i in range(PACK)}
+        res_sb = {(h, t): keep.tile([P, HALF], F32, name="res%d%d" % (h, t)) for h in range(HALVES) for t in range(N_TILES)}
+        mix = {(h, t): keep.tile([P, HALF], F32, name="mix%d%d" % (h, t)) for h in range(HALVES) for t in range(N_TILES)}
+
+        def codes_and_scales(name, width):
+            return (keep.tile([P, width], U32, name=name + "_codes", align_bytes=64),
+                    keep.tile([P, width], U8, name=name + "_scales", align_bytes=64))
+
+        w_mx = {(m, a): codes_and_scales("%s%d" % (m, a), N) for m in ("hi", "lo", "v") for a in range(PASSES)}
+        x_mx = {(a, h): codes_and_scales("x%d%d" % (a, h), HALF) for a in range(PASSES) for h in range(HALVES)}
+
+        def by_rows(ap):
+            return ap.rearrange("p i (c u) -> p c i u", u=4)
+
+        def by_words(ap):
+            return ap.rearrange("p (c u i) -> p c i u", u=4, i=PACK)
+
+        def quantize(mx, cols, packed):
+            nc.vector.quantize_mx(out=mx[0][:, cols].bitcast(FP8X4), scales=mx[1][:, cols], in_=packed)
+
+        raw = {}
+
+        def load_weight(name, w, a, cols):
+            width = cols.stop - cols.start
+            tile = keep.tile([P, PACK, width], F32, name="raw_%s%d_%d" % (name, a, cols.start))
+            rows = w[a * K_PASS:(a + 1) * K_PASS, :].rearrange("(p i) n -> p i n", i=PACK)
+            nc.sync.dma_start(out=tile[:], in_=rows[:, :, cols])
+            raw[name, a, cols.start] = tile
+
+        def load_plane(a, i):
+            rows = xT[a * K_PASS:(a + 1) * K_PASS, :].rearrange("(p i) t -> p i t", i=PACK)
+            nc.sync.dma_start(out=planes[a, i][:], in_=rows[:, i, :])
+
+        def load_res(h, t):
+            nc.sync.dma_start(out=res_sb[h, t][:], in_=res[t * P:(t + 1) * P, h * HALF:(h + 1) * HALF])
+
+        wk_pieces = [(0, slice(0, 128)), (0, slice(128, 256)), (0, slice(256, 512)), (1, slice(0, 256)), (1, slice(256, 512))]
+        whole = slice(0, N)
+
+        for a, cols in wk_pieces:
+            load_weight("k", wk, a, cols)
+        nc.sync.dma_start(offs_sb[:], offs)
+        nc.sync.dma_start(out=wgt_sb[:], in_=wgt)
+        for i in range(PACK):
+            load_plane(0, i)
+        load_weight("v", wv, 0, whole)
+        for i in range(PACK - 1):
+            load_plane(1, i)
+        load_weight("v", wv, 1, whole)
+        load_plane(1, PACK - 1)
+        with nc.allow_non_contiguous_dma(reason="one bias value a partition and output tile"):
+            nc.sync.dma_start(out=bg_sb[:], in_=bg.rearrange("(t p) -> p t", p=P))
+        for h in range(HALVES):
+            for t in range(N_TILES):
+                load_res(h, t)
+
+        hi_bf, lo_bf = {}, {}
+
+        def split_hi(a, cols):
+            width = cols.stop - cols.start
+            hi = keep.tile([P, width * PACK], BF16, name="hi%d_%d" % (a, cols.start), align_bytes=64)
+            upper = raw["k", a, cols.start][:].bitcast(BF16)[:, :, 1::2]
+            nc.scalar.copy(out=by_words(hi[:]), in_=by_rows(upper))
+            nc.vector.tensor_scalar(out=hi[:].bitcast(I32), in0=hi[:].bitcast(I32), scalar1=HI_MASK_PAIR, scalar2=None,
+                                    op0=ALU.bitwise_and)
+            hi_bf[a, cols.start] = hi
+
+        def split_lo(a, cols):
+            width = cols.stop - cols.start
+            lo = keep.tile([P, width * PACK], BF16, name="lo%d_%d" % (a, cols.start), align_bytes=64)
+            nc.vector.tensor_tensor(out=by_words(lo[:]), in0=by_rows(raw["k", a, cols.start][:]),
+                                    in1=by_words(hi_bf[a, cols.start][:]), op=ALU.subtract)
+            lo_bf[a, cols.start] = lo
+
+        count = len(wk_pieces)
+        for step in range(count + 2):
+            if step < count:
+                split_hi(*wk_pieces[step])
+            if 1 <= step <= count:
+                a, cols = wk_pieces[step - 1]
+                split_lo(a, cols)
+                quantize(w_mx["hi", a], cols, hi_bf[a, cols.start][:])
+            if step >= 2:
+                a, cols = wk_pieces[step - 2]
+                quantize(w_mx["lo", a], cols, lo_bf[a, cols.start][:])
+
+        picked, packed_x = {}, {}
+
+        def gather(a, i, h):
+            if i == 0:
+                picked[a, h] = ring.tile([P, PACK, HALF], F32, name="picked")
+            nc.vector.tensor_tensor(out=picked[a, h][:, i, :],
+                                    in0=planes[a, i][:].indirect(offs_sb[:, h * LIST_COLS:(h + 1) * LIST_COLS]),
+                                    in1=wgt_sb[:, h * HALF:(h + 1) * HALF], op=ALU.mult)
+
+        def pack_x(a, h):
+            packed_x[a, h] = ring.tile([P, HALF * PACK], BF16, name="packed_x", align_bytes=64)
+            nc.scalar.copy(out=by_words(packed_x[a, h][:]), in_=by_rows(picked[a, h][:]))
+
+        def quantize_x(a, h):
+            quantize(x_mx[a, h], slice(0, HALF), packed_x[a, h][:])
+
+        packed_v = {}
+
+        def pack_v(a):
+            packed_v[a] = keep.tile([P, N * PACK], BF16, name="packed_v%d" % a, align_bytes=64)
+            nc.scalar.copy(out=by_words(packed_v[a][:]), in_=by_rows(raw["v", a, 0][:]))
+
+        def quantize_v(a):
+            quantize(w_mx["v", a], whole, packed_v[a][:])
+
+        banks = {}
+
+        def product(m, a, h, t, start, stop):
+            kind = "v" if m == "v" else "k"
+            if start:
+                banks[kind, h, t] = psum.tile([P, HALF], F32, name="bank_%s%d" % (kind, t))
+            cols = slice(t * P, (t + 1) * P)
+            nc.tensor.matmul_mx(out=banks[kind, h, t][:],
+                                lhsT=w_mx[m, a][0][:, cols].bitcast(FP8X4), lhsT_scale=w_mx[m, a][1][:, cols],
+                                rhs=x_mx[a, h][0][:].bitcast(FP8X4), rhs_scale=x_mx[a, h][1][:],
+                                start=start, stop=stop)
+
+        def products(a, h, t):
+            product("hi", a, h, t, a == 0, False)
+            product("lo", a, h, t, False, a == PASSES - 1)
+            product("v", a, h, t, a == 0, a == PASSES - 1)
+
+        gate = {}
+
+        def make_gate(h, t):
+            gate[h, t] = gates.tile([P, HALF], F32, name="gate")
+            nc.scalar.activation(out=gate[h, t][:], in_=banks["k", h, t][:], func=ACT.Sigmoid, bias=bg_sb[:, t:t + 1])
+
+        def difference(h, t):
+            nc.vector.tensor_tensor(out=mix[h, t][:], in0=banks["v", h, t][:], in1=res_sb[h, t][:], op=ALU.subtract)
+
+        def gated(h, t):
+            nc.vector.tensor_tensor(out=mix[h, t][:], in0=mix[h, t][:], in1=gate[h, t][:], op=ALU.mult)
+
+        def finish(h, t):
+            nc.vector.tensor_tensor(out=mix[h, t][:], in0=mix[h, t][:], in1=res_sb[h, t][:], op=ALU.add)
+            nc.sync.dma_start(out=out[t * P:(t + 1) * P, h * HALF:(h + 1) * HALF], in_=mix[h, t][:])
+
+        for i in range(PACK):
+            gather(0, i, 0)
+            if i < PACK - 1:
+                gather(0, i, 1)
+        pack_x(0, 0)
+        gather(0, PACK - 1, 1)
+        pack_v(0)
+        pack_x(0, 1)
+        gather(1, 0, 0)
+        quantize_x(0, 0)
+        gather(1, 1, 0)
+        quantize_v(0)
+        for t in range(N_TILES):
+            products(0, 0, t)
+        gather(1, 2, 0)
+        quantize_x(0, 1)
+        pack_v(1)
+        gather(1, 3, 0)
+        pack_x(1, 0)
+        quantize_v(1)
+        gather(1, 0, 1)
+        gather(1, 1, 1)
+        quantize_x(1, 0)
+        for t in range(N_TILES):
+            products(1, 0, t)
+            make_gate(0, t)
+        gather(1, 2, 1)
+        gather(1, 3, 1)
+        pack_x(1, 1)
+
+        units = [(h, t) for h in range(HALVES) for t in range(N_TILES)]
+        for step in range(len(units) + 2):
+            if step < len(units):
+                h, t = units[step]
+                if h == 1:
+                    products(1, h, t)
+                    make_gate(h, t)
+                difference(h, t)
+                if h == 0:
+                    products(0, 1, t)
+                if step == 2:
+                    quantize_x(1, 1)
+            if 1 <= step <= len(units):
+                gated(*units[step - 1])
+            if step >= 2:
+                finish(*units[step - 2])

@@ -1,6 +1,7 @@
 from contextlib import ExitStack
 
 import concourse.mybir as mybir
+from concourse.masks import make_identity
 
 K, N, T, J = 1024, 512, 2048, 1024
 FLOPS = 3 * 2 * K * N * J
@@ -24,10 +25,31 @@ HALVES = J // HALF
 N_TILES = N // P
 LIST_COLS = HALF // 16
 HI_MASK_PAIR = 0xFFF0FFF0 - (1 << 32)
+HI_MASK = 0xFFF00000 - (1 << 32)
+SIGN_BIT = -(1 << 31)
 
 
 def tile_list_hl_hway_kernel(tc, xT, wgt, wk, wv, bg, res, offs, out):
     nc = tc.nc
+    LOADS = [("k0", 0), ("k0", 1), ("offs",), ("w", 0), ("x", 0, 0), ("k1",), ("w", 1), ("x", 0, 1), ("x", 0, 2), ("x", 0, 3), ("k0", 2),
+             ("x", 1, 0), ("x", 1, 1), ("x", 1, 2), ("bg",), ("v", 0, 0), ("v", 1, 0), ("x", 1, 3), ("v", 0, 1), ("v", 1, 1)] + [("r", h, t) for h in range(2) for t in range(4)]
+    UNITS = [(h, t) for h in range(2) for t in range(4)]
+    STEPS = ([("mask",), ("turn", 0), ("turn", 1), ("ret", 0), ("turn", 2), ("ret", 1), ("turn", 3), ("ret", 2), ("ret", 3), ("phi",)]
+             + [("g", 0, i, h, None) for i in range(4) for h in range(2)] + [("qhi",), ("qlo",), ("px", 0, 0, None), ("px", 0, 1, None),
+             ("g", 1, 0, 0, None), ("qx", 0, 0, None), ("g", 1, 1, 0, None), ("qx", 0, 1, None), ("pv", 0, 0), ("pv", 1, 0), ("g", 1, 2, 0, None),
+             ("qv", 0, 0), ("qv", 1, 0), ("g", 1, 3, 0, None), ("px", 1, 0, None)]
+             + [("mk", 0, 0, t) for t in range(4)] + [("mv", 0, 0, t) for t in range(2)]
+             + [("g", 1, i, 1, 0) for i in range(4)] + [("qx", 1, 0, None), ("pv", 0, 1), ("pv", 1, 1), ("px", 1, 1, 0)]
+             + [("g", 1, i, 1, 1) for i in range(4)] + [("qv", 0, 1), ("qv", 1, 1)]
+             + [("mk", 1, 0, 0), ("mv", 1, 0, 0), ("gate", 0, 0), ("px", 1, 1, 1), ("mk", 1, 0, 1), ("mv", 1, 0, 1), ("gate", 0, 1)]
+             + [s for t in range(2, 4) for s in (("mk", 1, 0, t), ("mv", 0, 0, t), ("mv", 1, 0, t), ("gate", 0, t))] + [("qx", 1, 1, 0)]
+             + [s for n in range(10) for s in (
+                 ([("mk", 1, 1, UNITS[n][1]), ("mv", 1, 1, UNITS[n][1]), ("gate",) + UNITS[n]] if 4 <= n < 8 else [])
+                 + ([("d",) + UNITS[n]] if n < 8 else [])
+                 + ([("mk", 0, 1, n), ("mv", 0, 1, n)] if n < 4 else [])
+                 + ([("qx", 1, 1, 1)] if n == 2 else [])
+                 + ([("t",) + UNITS[n - 1]] if 1 <= n <= 8 else [])
+                 + ([("f",) + UNITS[n - 2]] if n >= 2 else []))])
     with ExitStack() as ctx:
         keep = ctx.enter_context(tc.tile_pool(name="keep", bufs=1))
         ring = ctx.enter_context(tc.tile_pool(name="ring", bufs=3))
@@ -35,11 +57,11 @@ def tile_list_hl_hway_kernel(tc, xT, wgt, wk, wv, bg, res, offs, out):
         psum = ctx.enter_context(tc.psum_pool(name="psum", bufs=1))
 
         offs_sb = keep.tile([P, J // 16], U16, name="offs_sb")
-        wgt_sb = keep.tile([P, J], F32, name="wgt_sb")
+        wgt_sb = [keep.tile([P, HALF], F32, name="wgt0", tag="after_first_half", align_bytes=64), keep.tile([P, HALF], F32, name="wgt1")]
         bg_sb = keep.tile([P, N_TILES], F32, name="bg_sb")
         planes = {(a, i): keep.tile([P, T], F32, name="plane%d%d" % (a, i)) for a in range(PASSES) for i in range(PACK)}
         res_sb = {(h, t): keep.tile([P, HALF], F32, name="res%d%d" % (h, t)) for h in range(HALVES) for t in range(N_TILES)}
-        mix = {(h, t): keep.tile([P, HALF], F32, name="mix%d%d" % (h, t)) for h in range(HALVES) for t in range(N_TILES)}
+        mix = {}
 
         def codes_and_scales(name, width):
             return (keep.tile([P, width], U32, name=name + "_codes", align_bytes=64),
@@ -73,25 +95,37 @@ def tile_list_hl_hway_kernel(tc, xT, wgt, wk, wv, bg, res, offs, out):
         def load_res(h, t):
             nc.sync.dma_start(out=res_sb[h, t][:], in_=res[t * P:(t + 1) * P, h * HALF:(h + 1) * HALF])
 
-        wk_pieces = [(0, slice(0, 128)), (0, slice(128, 256)), (0, slice(256, 512)), (1, slice(0, 256)), (1, slice(256, 512))]
+        wk_pieces = [(0, slice(0, 128)), (0, slice(128, 384)), (0, slice(384, 512))]
         whole = slice(0, N)
 
-        for a, cols in wk_pieces:
-            load_weight("k", wk, a, cols)
-        nc.sync.dma_start(offs_sb[:], offs)
-        nc.sync.dma_start(out=wgt_sb[:], in_=wgt)
-        for i in range(PACK):
-            load_plane(0, i)
-        load_weight("v", wv, 0, whole)
-        for i in range(PACK - 1):
-            load_plane(1, i)
-        load_weight("v", wv, 1, whole)
-        load_plane(1, PACK - 1)
-        with nc.allow_non_contiguous_dma(reason="one bias value a partition and output tile"):
-            nc.sync.dma_start(out=bg_sb[:], in_=bg.rearrange("(t p) -> p t", p=P))
-        for h in range(HALVES):
-            for t in range(N_TILES):
-                load_res(h, t)
+        v_pieces = [slice(0, 256), slice(256, 512)]
+
+        warm = keep.tile([P, 1], F32, name="warm")
+        nc.vector.memset(warm[:], 0.0)
+        nc.scalar.activation(out=warm[:], in_=warm[:], func=ACT.Sigmoid)
+
+        def load(item):
+            kind = item[0]
+            if kind == "k0":
+                load_weight("k", wk, 0, wk_pieces[item[1]][1])
+            elif kind == "k1":
+                load_weight("k", wk, 1, whole)
+            elif kind == "v":
+                load_weight("v", wv, item[1], v_pieces[item[2]])
+            elif kind == "offs":
+                nc.sync.dma_start(offs_sb[:], offs)
+            elif kind == "w":
+                nc.sync.dma_start(out=wgt_sb[item[1]][:], in_=wgt[:, item[1] * HALF:(item[1] + 1) * HALF])
+            elif kind == "x":
+                load_plane(item[1], item[2])
+            elif kind == "bg":
+                with nc.allow_non_contiguous_dma(reason="one bias value a partition and output tile"):
+                    nc.sync.dma_start(out=bg_sb[:], in_=bg.rearrange("(t p) -> p t", p=P))
+            else:
+                load_res(item[1], item[2])
+
+        for item in LOADS:
+            load(item)
 
         hi_bf, lo_bf = {}, {}
 
@@ -123,30 +157,77 @@ def tile_list_hl_hway_kernel(tc, xT, wgt, wk, wv, bg, res, offs, out):
                 a, cols = wk_pieces[step - 2]
                 quantize(w_mx["lo", a], cols, lo_bf[a, cols.start][:])
 
+        identity = keep.tile([P, P], F32, name="identity")
+        make_identity(nc, identity[:])
+
+        neg_hi, lo_turned = {}, {}
+        tiles = [slice(t * P, (t + 1) * P) for t in range(N_TILES)]
+
+        def mask_hi(a):
+            neg_hi[a] = ring.tile([P, PACK, N], F32, name="neg_hi", bufs=1)
+            nc.vector.tensor_scalar(out=neg_hi[a][:].bitcast(I32), in0=raw["k", a, 0][:].bitcast(I32), scalar1=HI_MASK,
+                                    scalar2=SIGN_BIT, op0=ALU.bitwise_and, op1=ALU.bitwise_xor)
+
+        def pack_hi(a):
+            hi_bf[a] = ring.tile([P, N * PACK], BF16, name="hi_bf", align_bytes=64, bufs=1)
+            nc.scalar.activation(out=by_words(hi_bf[a][:]), in_=by_rows(neg_hi[a][:]), func=ACT.Copy, scale=-1.0)
+
+        def turn_lo(a, t):
+            bank = psum.tile([P, PACK, P], F32, name="bank_k%d" % t)
+            for i in range(PACK):
+                nc.tensor.matmul(bank[:, i, :], lhsT=raw["k", a, 0][:, i, tiles[t]], rhs=identity[:], start=True, stop=False,
+                                 is_transpose=True)
+                nc.tensor.matmul(bank[:, i, :], lhsT=neg_hi[a][:, i, tiles[t]], rhs=identity[:], start=False, stop=True,
+                                 is_transpose=True)
+            lo_turned[a, t] = ring.tile([P, PACK * P], BF16, name="lo_turned")
+            nc.scalar.copy(out=lo_turned[a, t][:].rearrange("n (u p e) -> n u p e", u=2, e=2),
+                           in_=bank[:].rearrange("n (u e) p -> n u p e", u=2))
+
+        def return_lo(a, t):
+            if t == 0:
+                lo_bf[a] = ring.tile([P, N * PACK], BF16, name="lo_bf", align_bytes=64, bufs=1)
+            bank = psum.tile([P, 2, P], F32, name="bank_v%d" % t)
+            words = lo_turned[a, t][:].bitcast(F32)
+            for u in range(2):
+                nc.tensor.transpose(bank[:, u, :], words[:, u * P:(u + 1) * P], identity[:])
+            nc.scalar.copy(out=lo_bf[a][:, t * P * PACK:(t + 1) * P * PACK].bitcast(F32).rearrange("p (n u) -> p n u", u=2),
+                           in_=bank[:].rearrange("p u n -> p n u"))
+
+        def make_lo(a):
+            for step in range(N_TILES + 1):
+                if step < N_TILES:
+                    turn_lo(a, step)
+                if step >= 1:
+                    return_lo(a, step - 1)
+
         picked, packed_x = {}, {}
 
-        def gather(a, i, h):
+        def gather(a, i, h, cols, tag="picked", pool=ring):
+            width = cols.stop - cols.start
             if i == 0:
-                picked[a, h] = ring.tile([P, PACK, HALF], F32, name="picked")
-            nc.vector.tensor_tensor(out=picked[a, h][:, i, :],
-                                    in0=planes[a, i][:].indirect(offs_sb[:, h * LIST_COLS:(h + 1) * LIST_COLS]),
-                                    in1=wgt_sb[:, h * HALF:(h + 1) * HALF], op=ALU.mult)
+                picked[a, h, cols.start] = pool.tile([P, PACK, width], F32, name="picked", tag=tag, align_bytes=64)
+            first = (h * HALF + cols.start) // 16
+            nc.vector.tensor_tensor(out=picked[a, h, cols.start][:, i, :],
+                                    in0=planes[a, i][:].indirect(offs_sb[:, first:first + width // 16]),
+                                    in1=wgt_sb[h][:, cols], op=ALU.mult)
 
-        def pack_x(a, h):
-            packed_x[a, h] = ring.tile([P, HALF * PACK], BF16, name="packed_x", align_bytes=64)
-            nc.scalar.copy(out=by_words(packed_x[a, h][:]), in_=by_rows(picked[a, h][:]))
+        def pack_x(a, h, cols, tag="packed_x", pool=ring):
+            width = cols.stop - cols.start
+            packed_x[a, h, cols.start] = pool.tile([P, width * PACK], BF16, name="packed_x", tag=tag, align_bytes=64)
+            nc.scalar.copy(out=by_words(packed_x[a, h, cols.start][:]), in_=by_rows(picked[a, h, cols.start][:]))
 
-        def quantize_x(a, h):
-            quantize(x_mx[a, h], slice(0, HALF), packed_x[a, h][:])
+        def quantize_x(a, h, cols):
+            quantize(x_mx[a, h], cols, packed_x[a, h, cols.start][:])
 
         packed_v = {}
 
-        def pack_v(a):
-            packed_v[a] = keep.tile([P, N * PACK], BF16, name="packed_v%d" % a, align_bytes=64)
-            nc.scalar.copy(out=by_words(packed_v[a][:]), in_=by_rows(raw["v", a, 0][:]))
+        def pack_v(a, cols):
+            width = cols.stop - cols.start
+            packed_v[a, cols.start] = keep.tile([P, width * PACK], BF16, name="packed_v%d_%d" % (a, cols.start), align_bytes=64)
+            nc.scalar.copy(out=by_words(packed_v[a, cols.start][:]), in_=by_rows(raw["v", a, cols.start][:]))
 
-        def quantize_v(a):
-            quantize(w_mx["v", a], whole, packed_v[a][:])
+        def quantize_v(a, cols):
+            quantize(w_mx["v", a], cols, packed_v[a, cols.start][:])
 
         banks = {}
 
@@ -172,6 +253,7 @@ def tile_list_hl_hway_kernel(tc, xT, wgt, wk, wv, bg, res, offs, out):
             nc.scalar.activation(out=gate[h, t][:], in_=banks["k", h, t][:], func=ACT.Sigmoid, bias=bg_sb[:, t:t + 1])
 
         def difference(h, t):
+            mix[h, t] = ring.tile([P, HALF], F32, name="mix", bufs=6)
             nc.vector.tensor_tensor(out=mix[h, t][:], in0=banks["v", h, t][:], in1=res_sb[h, t][:], op=ALU.subtract)
 
         def gated(h, t):
@@ -181,49 +263,56 @@ def tile_list_hl_hway_kernel(tc, xT, wgt, wk, wv, bg, res, offs, out):
             nc.vector.tensor_tensor(out=mix[h, t][:], in0=mix[h, t][:], in1=res_sb[h, t][:], op=ALU.add)
             nc.sync.dma_start(out=out[t * P:(t + 1) * P, h * HALF:(h + 1) * HALF], in_=mix[h, t][:])
 
-        for i in range(PACK):
-            gather(0, i, 0)
-            if i < PACK - 1:
-                gather(0, i, 1)
-        pack_x(0, 0)
-        gather(0, PACK - 1, 1)
-        pack_v(0)
-        pack_x(0, 1)
-        gather(1, 0, 0)
-        quantize_x(0, 0)
-        gather(1, 1, 0)
-        quantize_v(0)
-        for t in range(N_TILES):
-            products(0, 0, t)
-        gather(1, 2, 0)
-        quantize_x(0, 1)
-        pack_v(1)
-        gather(1, 3, 0)
-        pack_x(1, 0)
-        quantize_v(1)
-        gather(1, 0, 1)
-        gather(1, 1, 1)
-        quantize_x(1, 0)
-        for t in range(N_TILES):
-            products(1, 0, t)
-            make_gate(0, t)
-        gather(1, 2, 1)
-        gather(1, 3, 1)
-        pack_x(1, 1)
+        full = slice(0, HALF)
+        quarters = [slice(0, HALF // 2), slice(HALF // 2, HALF)]
+        def run(item):
+            kind, args = item[0], item[1:]
+            if kind == "g":
+                a, i, h, q = args
+                if q is None:
+                    gather(a, i, h, full)
+                else:
+                    gather(a, i, h, quarters[q], ("after_first_half", "after_first_codes")[q], keep)
+            elif kind == "px":
+                a, h, q = args
+                if (a, h) == (1, 0):
+                    pack_x(a, h, full, "after_first_codes", keep)
+                else:
+                    pack_x(a, h, full if q is None else quarters[q])
+            elif kind == "qx":
+                a, h, q = args
+                quantize_x(a, h, full if q is None else quarters[q])
+            elif kind == "pv":
+                pack_v(args[0], v_pieces[args[1]])
+            elif kind == "qv":
+                quantize_v(args[0], v_pieces[args[1]])
+            elif kind == "mask":
+                mask_hi(1)
+            elif kind == "turn":
+                turn_lo(1, args[0])
+            elif kind == "ret":
+                return_lo(1, args[0])
+            elif kind == "phi":
+                pack_hi(1)
+            elif kind == "qhi":
+                quantize(w_mx["hi", 1], whole, hi_bf[1][:])
+            elif kind == "qlo":
+                quantize(w_mx["lo", 1], whole, lo_bf[1][:])
+            elif kind == "mk":
+                a, h, t = args
+                product("hi", a, h, t, a == 0, False)
+                product("lo", a, h, t, False, a == PASSES - 1)
+            elif kind == "mv":
+                a, h, t = args
+                product("v", a, h, t, a == 0, a == PASSES - 1)
+            elif kind == "gate":
+                make_gate(*args)
+            elif kind == "d":
+                difference(*args)
+            elif kind == "t":
+                gated(*args)
+            else:
+                finish(*args)
 
-        units = [(h, t) for h in range(HALVES) for t in range(N_TILES)]
-        for step in range(len(units) + 2):
-            if step < len(units):
-                h, t = units[step]
-                if h == 1:
-                    products(1, h, t)
-                    make_gate(h, t)
-                difference(h, t)
-                if h == 0:
-                    products(0, 1, t)
-                if step == 2:
-                    quantize_x(1, 1)
-            if 1 <= step <= len(units):
-                gated(*units[step - 1])
-            if step >= 2:
-                finish(*units[step - 2])
+        for item in STEPS:
+            run(item)

@@ -17,302 +17,295 @@ ALU = mybir.AluOpType
 ACT = mybir.ActivationFunctionType
 
 P = 128
-PACK = 4
-K_PASS = P * PACK
+PLANES = 4
+K_PASS = P * PLANES
 PASSES = K // K_PASS
 HALF = 512
-HALVES = J // HALF
 N_TILES = N // P
-LIST_COLS = HALF // 16
-HI_MASK_PAIR = 0xFFF0FFF0 - (1 << 32)
+UNITS = (J // HALF) * N_TILES
+GROUP = 16
+RUN = 4
+ALIGN = 64
+
 HI_MASK = 0xFFF00000 - (1 << 32)
+HI_MASK_PAIR = 0xFFF0FFF0 - (1 << 32)
 SIGN_BIT = -(1 << 31)
+
+WK0_PIECES = (slice(0, 128), slice(128, 256), slice(256, 512))
+LEFT, RIGHT = slice(0, N // 2), slice(N // 2, N)
+QUARTERS = (slice(0, HALF // 2), slice(HALF // 2, HALF))
+
+KE_BANK = (0, 1, 2, 3, 0, 2, 4, 2)
+VE_BANK = (4, 5, 6, 7, 1, 3, 5, 0)
+ON_GPSIMD = (1, 3, 4, 5, 6)
 
 
 def tile_list_hl_hway_kernel(tc, xT, wgt, wk, wv, bg, res, offs, out):
     nc = tc.nc
-    LOADS = [("k0", 0), ("k0", 1), ("offs",), ("w", 0), ("x", 0, 0), ("k1",), ("w", 1), ("x", 0, 1), ("x", 0, 2), ("x", 0, 3), ("k0", 2),
-             ("x", 1, 0), ("x", 1, 1), ("x", 1, 2), ("bg",), ("v", 0, 0), ("v", 1, 0), ("x", 1, 3), ("v", 0, 1), ("v", 1, 1)] + [("r", h, t) for h in range(2) for t in range(4)]
-    UNITS = [(h, t) for h in range(2) for t in range(4)]
-    STEPS = ([("mask",), ("turn", 0), ("turn", 1), ("ret", 0), ("turn", 2), ("ret", 1), ("turn", 3), ("ret", 2), ("ret", 3), ("phi",)]
-             + [("g", 0, i, h, None) for i in range(4) for h in range(2)] + [("qhi",), ("qlo",), ("px", 0, 0, None), ("px", 0, 1, None),
-             ("g", 1, 0, 0, None), ("qx", 0, 0, None), ("g", 1, 1, 0, None), ("qx", 0, 1, None), ("pv", 0, 0), ("pv", 1, 0), ("g", 1, 2, 0, None),
-             ("qv", 0, 0), ("qv", 1, 0), ("g", 1, 3, 0, None), ("px", 1, 0, None)]
-             + [("mk", 0, 0, t) for t in range(4)] + [("mv", 0, 0, t) for t in range(2)]
-             + [("g", 1, i, 1, 0) for i in range(4)] + [("qx", 1, 0, None), ("pv", 0, 1), ("pv", 1, 1), ("px", 1, 1, 0)]
-             + [("g", 1, i, 1, 1) for i in range(4)] + [("qv", 0, 1), ("qv", 1, 1)]
-             + [("mk", 1, 0, 0), ("mv", 1, 0, 0), ("gate", 0, 0), ("px", 1, 1, 1), ("mk", 1, 0, 1), ("mv", 1, 0, 1), ("gate", 0, 1)]
-             + [s for t in range(2, 4) for s in (("mk", 1, 0, t), ("mv", 0, 0, t), ("mv", 1, 0, t), ("gate", 0, t))] + [("qx", 1, 1, 0)]
-             + [s for n in range(10) for s in (
-                 ([("mk", 1, 1, UNITS[n][1]), ("mv", 1, 1, UNITS[n][1]), ("gate",) + UNITS[n]] if 4 <= n < 8 else [])
-                 + ([("d",) + UNITS[n]] if n < 8 else [])
-                 + ([("mk", 0, 1, n), ("mv", 0, 1, n)] if n < 4 else [])
-                 + ([("qx", 1, 1, 1)] if n == 2 else [])
-                 + ([("t",) + UNITS[n - 1]] if 1 <= n <= 8 else [])
-                 + ([("f",) + UNITS[n - 2]] if n >= 2 else []))])
     with ExitStack() as ctx:
         keep = ctx.enter_context(tc.tile_pool(name="keep", bufs=1))
-        ring = ctx.enter_context(tc.tile_pool(name="ring", bufs=3))
-        gates = ctx.enter_context(tc.tile_pool(name="gates", bufs=4))
+        ring = ctx.enter_context(tc.tile_pool(name="ring", bufs=2))
+        mixes = ctx.enter_context(tc.tile_pool(name="mixes", bufs=4))
         psum = ctx.enter_context(tc.psum_pool(name="psum", bufs=1))
 
-        offs_sb = keep.tile([P, J // 16], U16, name="offs_sb")
-        wgt_sb = [keep.tile([P, HALF], F32, name="wgt0", tag="after_first_half", align_bytes=64), keep.tile([P, HALF], F32, name="wgt1")]
-        bg_sb = keep.tile([P, N_TILES], F32, name="bg_sb")
-        planes = {(a, i): keep.tile([P, T], F32, name="plane%d%d" % (a, i)) for a in range(PASSES) for i in range(PACK)}
-        res_sb = {(h, t): keep.tile([P, HALF], F32, name="res%d%d" % (h, t)) for h in range(HALVES) for t in range(N_TILES)}
-        mix = {}
+        def width(cols):
+            return cols.stop - cols.start
 
-        def codes_and_scales(name, width):
-            return (keep.tile([P, width], U32, name=name + "_codes", align_bytes=64),
-                    keep.tile([P, width], U8, name=name + "_scales", align_bytes=64))
+        def n_tile(t):
+            return slice(t * P, (t + 1) * P)
 
-        w_mx = {(m, a): codes_and_scales("%s%d" % (m, a), N) for m in ("hi", "lo", "v") for a in range(PASSES)}
-        x_mx = {(a, h): codes_and_scales("x%d%d" % (a, h), HALF) for a in range(PASSES) for h in range(HALVES)}
+        def j_half(h):
+            return slice(h * HALF, (h + 1) * HALF)
 
-        def by_rows(ap):
-            return ap.rearrange("p i (c u) -> p c i u", u=4)
+        def by_planes(ap):
+            return ap.rearrange("p i (c u) -> p c i u", u=RUN)
 
-        def by_words(ap):
-            return ap.rearrange("p (c u i) -> p c i u", u=4, i=PACK)
+        def as_packed(ap):
+            return ap.rearrange("p (c u i) -> p c i u", u=RUN, i=PLANES)
+
+        def codes_and_scales(name, columns):
+            return (keep.tile([P, columns], U32, name=name + "_codes", align_bytes=ALIGN),
+                    keep.tile([P, columns], U8, name=name + "_scales", align_bytes=ALIGN))
 
         def quantize(mx, cols, packed):
-            nc.vector.quantize_mx(out=mx[0][:, cols].bitcast(FP8X4), scales=mx[1][:, cols], in_=packed)
+            codes, scales = mx
+            nc.vector.quantize_mx(out=codes[:, cols].bitcast(FP8X4), scales=scales[:, cols], in_=packed[:])
 
-        raw = {}
+        def bank(number, shape):
+            return psum.tile(shape, F32, name="bank%d" % number)
 
-        def load_weight(name, w, a, cols):
-            width = cols.stop - cols.start
-            tile = keep.tile([P, PACK, width], F32, name="raw_%s%d_%d" % (name, a, cols.start))
-            rows = w[a * K_PASS:(a + 1) * K_PASS, :].rearrange("(p i) n -> p i n", i=PACK)
-            nc.sync.dma_start(out=tile[:], in_=rows[:, :, cols])
-            raw[name, a, cols.start] = tile
-
-        def load_plane(a, i):
-            rows = xT[a * K_PASS:(a + 1) * K_PASS, :].rearrange("(p i) t -> p i t", i=PACK)
-            nc.sync.dma_start(out=planes[a, i][:], in_=rows[:, i, :])
-
-        def load_res(h, t):
-            nc.sync.dma_start(out=res_sb[h, t][:], in_=res[t * P:(t + 1) * P, h * HALF:(h + 1) * HALF])
-
-        wk_pieces = [(0, slice(0, 128)), (0, slice(128, 384)), (0, slice(384, 512))]
-        whole = slice(0, N)
-
-        v_pieces = [slice(0, 256), slice(256, 512)]
+        offs_sb = keep.tile([P, J // GROUP], U16, name="offs_sb")
+        wgt_sb = [keep.tile([P, HALF], F32, name="wgt%d" % h, align_bytes=ALIGN) for h in range(J // HALF)]
+        bg_sb = keep.tile([P, N_TILES], F32, name="bg_sb")
+        planes = {(a, i): keep.tile([P, T], F32, name="plane%d%d" % (a, i)) for a in range(PASSES) for i in range(PLANES)}
+        res_sb = [keep.tile([P, HALF], F32, name="res%d" % u, align_bytes=ALIGN) for u in range(UNITS)]
+        w_mx = {(m, a): codes_and_scales("%s%d" % (m, a), N) for m in ("hi", "lo", "v") for a in range(PASSES)}
+        x_mx = {(a, h): codes_and_scales("x%d%d" % (a, h), HALF) for a in range(PASSES) for h in range(J // HALF)}
 
         warm = keep.tile([P, 1], F32, name="warm")
         nc.vector.memset(warm[:], 0.0)
         nc.scalar.activation(out=warm[:], in_=warm[:], func=ACT.Sigmoid)
 
-        def load(item):
-            kind = item[0]
-            if kind == "k0":
-                load_weight("k", wk, 0, wk_pieces[item[1]][1])
-            elif kind == "k1":
-                load_weight("k", wk, 1, whole)
-            elif kind == "v":
-                load_weight("v", wv, item[1], v_pieces[item[2]])
-            elif kind == "offs":
-                nc.sync.dma_start(offs_sb[:], offs)
-            elif kind == "w":
-                nc.sync.dma_start(out=wgt_sb[item[1]][:], in_=wgt[:, item[1] * HALF:(item[1] + 1) * HALF])
-            elif kind == "x":
-                load_plane(item[1], item[2])
-            elif kind == "bg":
-                with nc.allow_non_contiguous_dma(reason="one bias value a partition and output tile"):
-                    nc.sync.dma_start(out=bg_sb[:], in_=bg.rearrange("(t p) -> p t", p=P))
-            else:
-                load_res(item[1], item[2])
+        def load_weight(name, w, a, cols):
+            tile = keep.tile([P, PLANES, width(cols)], F32, name="%s%d_%d" % (name, a, cols.start))
+            rows = w[a * K_PASS:(a + 1) * K_PASS, :].rearrange("(p i) n -> p i n", i=PLANES)
+            nc.sync.dma_start(out=tile[:], in_=rows[:, :, cols])
+            return tile
 
-        for item in LOADS:
-            load(item)
+        def load_plane(a, i):
+            rows = xT[a * K_PASS:(a + 1) * K_PASS, :].rearrange("(p i) t -> p i t", i=PLANES)
+            nc.sync.dma_start(out=planes[a, i][:], in_=rows[:, i, :])
 
-        hi_bf, lo_bf = {}, {}
+        wk0 = [load_weight("wk", wk, 0, cols) for cols in WK0_PIECES]
+        nc.sync.dma_start(offs_sb[:], offs)
+        nc.sync.dma_start(out=wgt_sb[0][:], in_=wgt[:, j_half(0)])
+        load_plane(0, 0)
+        wk1 = load_weight("wk", wk, 1, slice(0, N))
+        nc.sync.dma_start(out=wgt_sb[1][:], in_=wgt[:, j_half(1)])
+        for i in range(1, PLANES):
+            load_plane(0, i)
+        for i in range(PLANES - 1):
+            load_plane(1, i)
+        wv_left = [load_weight("wv", wv, a, LEFT) for a in range(PASSES)]
+        load_plane(1, PLANES - 1)
+        wv_right = [load_weight("wv", wv, a, RIGHT) for a in range(PASSES)]
+        with nc.allow_non_contiguous_dma(reason="one bias value for each partition and n-tile"):
+            nc.sync.dma_start(out=bg_sb[:], in_=bg.rearrange("(t p) -> p t", p=P))
+        for u in range(UNITS):
+            nc.sync.dma_start(out=res_sb[u][:], in_=res[n_tile(u % N_TILES), j_half(u // N_TILES)])
 
-        def split_hi(a, cols):
-            width = cols.stop - cols.start
-            hi = keep.tile([P, width * PACK], BF16, name="hi%d_%d" % (a, cols.start), align_bytes=64)
-            upper = raw["k", a, cols.start][:].bitcast(BF16)[:, :, 1::2]
-            nc.scalar.copy(out=by_words(hi[:]), in_=by_rows(upper))
+        hi0, lo0 = [], []
+
+        def split_hi0(n):
+            hi = keep.tile([P, width(WK0_PIECES[n]) * PLANES], BF16, name="hi0_%d" % n, align_bytes=ALIGN)
+            nc.scalar.copy(out=as_packed(hi[:]), in_=by_planes(wk0[n][:].bitcast(BF16)[:, :, 1::2]))
             nc.vector.tensor_scalar(out=hi[:].bitcast(I32), in0=hi[:].bitcast(I32), scalar1=HI_MASK_PAIR, scalar2=None,
                                     op0=ALU.bitwise_and)
-            hi_bf[a, cols.start] = hi
+            hi0.append(hi)
 
-        def split_lo(a, cols):
-            width = cols.stop - cols.start
-            lo = keep.tile([P, width * PACK], BF16, name="lo%d_%d" % (a, cols.start), align_bytes=64)
-            nc.vector.tensor_tensor(out=by_words(lo[:]), in0=by_rows(raw["k", a, cols.start][:]),
-                                    in1=by_words(hi_bf[a, cols.start][:]), op=ALU.subtract)
-            lo_bf[a, cols.start] = lo
+        def split_lo0(n):
+            lo = keep.tile([P, width(WK0_PIECES[n]) * PLANES], BF16, name="lo0_%d" % n, align_bytes=ALIGN)
+            nc.vector.tensor_tensor(out=as_packed(lo[:]), in0=by_planes(wk0[n][:]), in1=as_packed(hi0[n][:]), op=ALU.subtract)
+            lo0.append(lo)
 
-        count = len(wk_pieces)
-        for step in range(count + 2):
-            if step < count:
-                split_hi(*wk_pieces[step])
-            if 1 <= step <= count:
-                a, cols = wk_pieces[step - 1]
-                split_lo(a, cols)
-                quantize(w_mx["hi", a], cols, hi_bf[a, cols.start][:])
+        pieces = len(WK0_PIECES)
+        for step in range(pieces + 2):
+            if step < pieces:
+                split_hi0(step)
+            if 1 <= step <= pieces:
+                split_lo0(step - 1)
+                quantize(w_mx["hi", 0], WK0_PIECES[step - 1], hi0[step - 1])
             if step >= 2:
-                a, cols = wk_pieces[step - 2]
-                quantize(w_mx["lo", a], cols, lo_bf[a, cols.start][:])
+                quantize(w_mx["lo", 0], WK0_PIECES[step - 2], lo0[step - 2])
+
+        neg_bg = keep.tile([P, N_TILES], F32, name="neg_bg")
+        nc.scalar.activation(out=neg_bg[:], in_=bg_sb[:], func=ACT.Copy, scale=-1.0)
 
         identity = keep.tile([P, P], F32, name="identity")
         make_identity(nc, identity[:])
 
-        neg_hi, lo_turned = {}, {}
-        tiles = [slice(t * P, (t + 1) * P) for t in range(N_TILES)]
+        neg_hi1 = keep.tile([P, PLANES, N], F32, name="neg_hi1")
+        nc.vector.tensor_scalar(out=neg_hi1[:].bitcast(I32), in0=wk1[:].bitcast(I32), scalar1=HI_MASK, scalar2=SIGN_BIT,
+                                op0=ALU.bitwise_and, op1=ALU.bitwise_xor)
+        lo1 = keep.tile([P, N * PLANES], BF16, name="lo1", align_bytes=ALIGN)
+        lo1_turned = []
 
-        def mask_hi(a):
-            neg_hi[a] = ring.tile([P, PACK, N], F32, name="neg_hi", bufs=1)
-            nc.vector.tensor_scalar(out=neg_hi[a][:].bitcast(I32), in0=raw["k", a, 0][:].bitcast(I32), scalar1=HI_MASK,
-                                    scalar2=SIGN_BIT, op0=ALU.bitwise_and, op1=ALU.bitwise_xor)
-
-        def pack_hi(a):
-            hi_bf[a] = ring.tile([P, N * PACK], BF16, name="hi_bf", align_bytes=64, bufs=1)
-            nc.scalar.activation(out=by_words(hi_bf[a][:]), in_=by_rows(neg_hi[a][:]), func=ACT.Copy, scale=-1.0)
-
-        def turn_lo(a, t):
-            bank = psum.tile([P, PACK, P], F32, name="bank_k%d" % t)
-            for i in range(PACK):
-                nc.tensor.matmul(bank[:, i, :], lhsT=raw["k", a, 0][:, i, tiles[t]], rhs=identity[:], start=True, stop=False,
+        def turn_lo1(t):
+            sums = bank(KE_BANK[t], [P, PLANES, P])
+            for i in range(PLANES):
+                nc.tensor.matmul(sums[:, i, :], lhsT=wk1[:, i, n_tile(t)], rhs=identity[:], start=True, stop=False,
                                  is_transpose=True)
-                nc.tensor.matmul(bank[:, i, :], lhsT=neg_hi[a][:, i, tiles[t]], rhs=identity[:], start=False, stop=True,
+                nc.tensor.matmul(sums[:, i, :], lhsT=neg_hi1[:, i, n_tile(t)], rhs=identity[:], start=False, stop=True,
                                  is_transpose=True)
-            lo_turned[a, t] = ring.tile([P, PACK * P], BF16, name="lo_turned")
-            nc.scalar.copy(out=lo_turned[a, t][:].rearrange("n (u p e) -> n u p e", u=2, e=2),
-                           in_=bank[:].rearrange("n (u e) p -> n u p e", u=2))
+            turned = ring.tile([P, PLANES * P], BF16, name="lo1_turned")
+            nc.scalar.copy(out=turned[:].rearrange("n (u p e) -> n u p e", u=2, e=2),
+                           in_=sums[:].rearrange("n (u e) p -> n u p e", u=2))
+            lo1_turned.append(turned)
 
-        def return_lo(a, t):
-            if t == 0:
-                lo_bf[a] = ring.tile([P, N * PACK], BF16, name="lo_bf", align_bytes=64, bufs=1)
-            bank = psum.tile([P, 2, P], F32, name="bank_v%d" % t)
-            words = lo_turned[a, t][:].bitcast(F32)
+        def return_lo1(t):
+            back = bank(VE_BANK[t], [P, 2, P])
+            words = lo1_turned[t][:].bitcast(F32)
             for u in range(2):
-                nc.tensor.transpose(bank[:, u, :], words[:, u * P:(u + 1) * P], identity[:])
-            nc.scalar.copy(out=lo_bf[a][:, t * P * PACK:(t + 1) * P * PACK].bitcast(F32).rearrange("p (n u) -> p n u", u=2),
-                           in_=bank[:].rearrange("p u n -> p n u"))
+                nc.tensor.transpose(back[:, u, :], words[:, n_tile(u)], identity[:])
+            packed_words = lo1[:, t * P * PLANES:(t + 1) * P * PLANES].bitcast(F32)
+            nc.scalar.copy(out=packed_words.rearrange("p (n u) -> p n u", u=2), in_=back[:].rearrange("p u n -> p n u"))
 
-        def make_lo(a):
-            for step in range(N_TILES + 1):
-                if step < N_TILES:
-                    turn_lo(a, step)
-                if step >= 1:
-                    return_lo(a, step - 1)
+        for step in range(N_TILES + 1):
+            if step < N_TILES:
+                turn_lo1(step)
+            if step >= 1:
+                return_lo1(step - 1)
+        hi1 = keep.tile([P, N * PLANES], BF16, name="hi1", align_bytes=ALIGN)
+        nc.scalar.activation(out=as_packed(hi1[:]), in_=by_planes(neg_hi1[:]), func=ACT.Copy, scale=-1.0)
 
-        picked, packed_x = {}, {}
+        def picks(pool, cols, tag):
+            return pool.tile([P, PLANES, width(cols)], F32, name="picked", tag=tag, align_bytes=ALIGN)
 
-        def gather(a, i, h, cols, tag="picked", pool=ring):
-            width = cols.stop - cols.start
-            if i == 0:
-                picked[a, h, cols.start] = pool.tile([P, PACK, width], F32, name="picked", tag=tag, align_bytes=64)
-            first = (h * HALF + cols.start) // 16
-            nc.vector.tensor_tensor(out=picked[a, h, cols.start][:, i, :],
-                                    in0=planes[a, i][:].indirect(offs_sb[:, first:first + width // 16]),
+        def gather(picked, a, i, h, cols):
+            first = (h * HALF + cols.start) // GROUP
+            nc.vector.tensor_tensor(out=picked[:, i, :],
+                                    in0=planes[a, i][:].indirect(offs_sb[:, first:first + width(cols) // GROUP]),
                                     in1=wgt_sb[h][:, cols], op=ALU.mult)
 
-        def pack_x(a, h, cols, tag="packed_x", pool=ring):
-            width = cols.stop - cols.start
-            packed_x[a, h, cols.start] = pool.tile([P, width * PACK], BF16, name="packed_x", tag=tag, align_bytes=64)
-            nc.scalar.copy(out=by_words(packed_x[a, h, cols.start][:]), in_=by_rows(picked[a, h, cols.start][:]))
+        def pack(pool, source, name):
+            packed = pool.tile([P, source.shape[2] * PLANES], BF16, name=name, align_bytes=ALIGN)
+            nc.scalar.copy(out=as_packed(packed[:]), in_=by_planes(source[:]))
+            return packed
 
-        def quantize_x(a, h, cols):
-            quantize(x_mx[a, h], cols, packed_x[a, h, cols.start][:])
+        ke, ve = {}, {}
 
-        packed_v = {}
+        def product(sums, m, a, u, start, stop):
+            w_codes, w_scales = w_mx[m, a]
+            x_codes, x_scales = x_mx[a, u // N_TILES]
+            cols = n_tile(u % N_TILES)
+            nc.tensor.matmul_mx(out=sums[:], lhsT=w_codes[:, cols].bitcast(FP8X4), lhsT_scale=w_scales[:, cols],
+                                rhs=x_codes[:].bitcast(FP8X4), rhs_scale=x_scales[:], start=start, stop=stop)
 
-        def pack_v(a, cols):
-            width = cols.stop - cols.start
-            packed_v[a, cols.start] = keep.tile([P, width * PACK], BF16, name="packed_v%d_%d" % (a, cols.start), align_bytes=64)
-            nc.scalar.copy(out=by_words(packed_v[a, cols.start][:]), in_=by_rows(raw["v", a, cols.start][:]))
+        def ke_pass(a, u):
+            if a == 0:
+                ke[u] = bank(KE_BANK[u], [P, HALF])
+            product(ke[u], "hi", a, u, a == 0, False)
+            product(ke[u], "lo", a, u, False, a == PASSES - 1)
 
-        def quantize_v(a, cols):
-            quantize(w_mx["v", a], cols, packed_v[a, cols.start][:])
-
-        banks = {}
-
-        def product(m, a, h, t, start, stop):
-            kind = "v" if m == "v" else "k"
-            if start:
-                banks[kind, h, t] = psum.tile([P, HALF], F32, name="bank_%s%d" % (kind, t))
-            cols = slice(t * P, (t + 1) * P)
-            nc.tensor.matmul_mx(out=banks[kind, h, t][:],
-                                lhsT=w_mx[m, a][0][:, cols].bitcast(FP8X4), lhsT_scale=w_mx[m, a][1][:, cols],
-                                rhs=x_mx[a, h][0][:].bitcast(FP8X4), rhs_scale=x_mx[a, h][1][:],
-                                start=start, stop=stop)
-
-        def products(a, h, t):
-            product("hi", a, h, t, a == 0, False)
-            product("lo", a, h, t, False, a == PASSES - 1)
-            product("v", a, h, t, a == 0, a == PASSES - 1)
-
-        gate = {}
-
-        def make_gate(h, t):
-            gate[h, t] = gates.tile([P, HALF], F32, name="gate")
-            nc.scalar.activation(out=gate[h, t][:], in_=banks["k", h, t][:], func=ACT.Sigmoid, bias=bg_sb[:, t:t + 1])
-
-        def difference(h, t):
-            mix[h, t] = ring.tile([P, HALF], F32, name="mix", bufs=6)
-            nc.vector.tensor_tensor(out=mix[h, t][:], in0=banks["v", h, t][:], in1=res_sb[h, t][:], op=ALU.subtract)
-
-        def gated(h, t):
-            nc.vector.tensor_tensor(out=mix[h, t][:], in0=mix[h, t][:], in1=gate[h, t][:], op=ALU.mult)
-
-        def finish(h, t):
-            nc.vector.tensor_tensor(out=mix[h, t][:], in0=mix[h, t][:], in1=res_sb[h, t][:], op=ALU.add)
-            nc.sync.dma_start(out=out[t * P:(t + 1) * P, h * HALF:(h + 1) * HALF], in_=mix[h, t][:])
+        def ve_pass(a, u):
+            if a == 0:
+                ve[u] = bank(VE_BANK[u], [P, HALF])
+            product(ve[u], "v", a, u, a == 0, a == PASSES - 1)
 
         full = slice(0, HALF)
-        quarters = [slice(0, HALF // 2), slice(HALF // 2, HALF)]
-        def run(item):
-            kind, args = item[0], item[1:]
-            if kind == "g":
-                a, i, h, q = args
-                if q is None:
-                    gather(a, i, h, full)
-                else:
-                    gather(a, i, h, quarters[q], ("after_first_half", "after_first_codes")[q], keep)
-            elif kind == "px":
-                a, h, q = args
-                if (a, h) == (1, 0):
-                    pack_x(a, h, full, "after_first_codes", keep)
-                else:
-                    pack_x(a, h, full if q is None else quarters[q])
-            elif kind == "qx":
-                a, h, q = args
-                quantize_x(a, h, full if q is None else quarters[q])
-            elif kind == "pv":
-                pack_v(args[0], v_pieces[args[1]])
-            elif kind == "qv":
-                quantize_v(args[0], v_pieces[args[1]])
-            elif kind == "mask":
-                mask_hi(1)
-            elif kind == "turn":
-                turn_lo(1, args[0])
-            elif kind == "ret":
-                return_lo(1, args[0])
-            elif kind == "phi":
-                pack_hi(1)
-            elif kind == "qhi":
-                quantize(w_mx["hi", 1], whole, hi_bf[1][:])
-            elif kind == "qlo":
-                quantize(w_mx["lo", 1], whole, lo_bf[1][:])
-            elif kind == "mk":
-                a, h, t = args
-                product("hi", a, h, t, a == 0, False)
-                product("lo", a, h, t, False, a == PASSES - 1)
-            elif kind == "mv":
-                a, h, t = args
-                product("v", a, h, t, a == 0, a == PASSES - 1)
-            elif kind == "gate":
-                make_gate(*args)
-            elif kind == "d":
-                difference(*args)
-            elif kind == "t":
-                gated(*args)
-            else:
-                finish(*args)
+        picked0 = [picks(ring, full, "picked") for h in range(J // HALF)]
+        for i in range(PLANES):
+            for h in range(J // HALF):
+                gather(picked0[h], 0, i, h, full)
+        quantize(w_mx["hi", 1], slice(0, N), hi1)
+        quantize(w_mx["lo", 1], slice(0, N), lo1)
+        packed0 = [pack(ring, picked0[h], "packed_x") for h in range(J // HALF)]
 
-        for item in STEPS:
-            run(item)
+        picked1 = picks(keep, full, "picked1")
+        for h in range(J // HALF):
+            gather(picked1, 1, h, 0, full)
+            quantize(x_mx[0, h], full, packed0[h])
+        packed_v = [pack(keep, wv_left[a], "packed_v_left%d" % a) for a in range(PASSES)]
+        gather(picked1, 1, PLANES - 2, 0, full)
+        for a in range(PASSES):
+            quantize(w_mx["v", a], LEFT, packed_v[a])
+        gather(picked1, 1, PLANES - 1, 0, full)
+        packed1 = pack(ring, picked1, "packed_x")
+        left_units = range(LEFT.stop // P)
+        for u in range(N_TILES):
+            ke_pass(0, u)
+        for u in left_units:
+            ve_pass(0, u)
+
+        quarter0 = picks(keep, QUARTERS[0], "wgt0")
+        for i in range(PLANES):
+            gather(quarter0, 1, i, 1, QUARTERS[0])
+        quantize(x_mx[1, 0], full, packed1)
+        packed_v = [pack(keep, wv_right[a], "packed_v_right%d" % a) for a in range(PASSES)]
+        packed_quarter0 = pack(ring, quarter0, "packed_x")
+        quarter1 = picks(keep, QUARTERS[1], "picked1")
+        for i in range(PLANES):
+            gather(quarter1, 1, i, 1, QUARTERS[1])
+        for a in range(PASSES):
+            quantize(w_mx["v", a], RIGHT, packed_v[a])
+        packed_quarter1 = pack(ring, quarter1, "packed_x")
+        quantize(x_mx[1, 1], QUARTERS[0], packed_quarter0)
+        quantize(x_mx[1, 1], QUARTERS[1], packed_quarter1)
+
+        carry, mix = {}, {}
+
+        def unit_tile(name, slot):
+            return keep.tile([P, HALF], F32, name=name, tag=slot, align_bytes=ALIGN)
+
+        def make_carry(u):
+            t = u % N_TILES
+            carry[u] = unit_tile("carry", "carry%d" % u)
+            nc.scalar.activation(out=carry[u][:], in_=ke[u][:], func=ACT.Sigmoid, bias=neg_bg[:, t:t + 1], scale=-1.0)
+
+        def difference(u, slot=None):
+            mix[u] = unit_tile("mix", slot) if slot else mixes.tile([P, HALF], F32, name="mix")
+            nc.vector.tensor_tensor(out=mix[u][:], in0=ve[u][:], in1=res_sb[u][:], op=ALU.subtract)
+
+        def weigh(u):
+            engine = nc.gpsimd if u in ON_GPSIMD else nc.vector
+            engine.tensor_tensor(out=mix[u][:], in0=mix[u][:], in1=carry[u][:], op=ALU.mult)
+
+        def finish(u, slot=None):
+            result = unit_tile("result", slot) if slot else mix[u]
+            nc.vector.tensor_tensor(out=result[:], in0=ve[u][:], in1=mix[u][:], op=ALU.subtract)
+            nc.sync.dma_start(out=out[n_tile(u % N_TILES), j_half(u // N_TILES)], in_=result[:])
+
+        for u in range(N_TILES):
+            ke_pass(1, u)
+            if u not in left_units:
+                ve_pass(0, u)
+            ve_pass(1, u)
+            make_carry(u)
+
+        difference(0)
+        difference(1)
+        weigh(0)
+        weigh(1)
+        difference(2, "carry0")
+        finish(0)
+        difference(3, "res2")
+        weigh(2)
+        weigh(3)
+        finish(1)
+
+        last = UNITS - 1
+        for u in range(N_TILES, UNITS):
+            if u == last:
+                for a in range(PASSES):
+                    ve_pass(a, u)
+            for a in range(PASSES):
+                ke_pass(a, u)
+            make_carry(u)
+            if u != last:
+                for a in range(PASSES):
+                    ve_pass(a, u)
+            difference(u)
+            finish(u - 2, "res%d" % u)
+            weigh(u)
+        finish(last - 1, "carry%d" % last)
+        finish(last)

from contextlib import ExitStack

import concourse.mybir as mybir
from concourse.masks import make_identity

K, N, T, J = 1024, 512, 2048, 1024
FLOPS = 3 * 2 * K * N * J

F32 = mybir.dt.float32
BF16 = mybir.dt.bfloat16
I32 = mybir.dt.int32
U32 = mybir.dt.uint32
U16 = mybir.dt.uint16
U8 = mybir.dt.uint8
FP8X4 = mybir.dt.float8_e4m3fn_x4
ALU = mybir.AluOpType
ACT = mybir.ActivationFunctionType

P = 128
PLANES = 4
K_PASS = P * PLANES
PASSES = K // K_PASS
HALF = 512
N_TILES = N // P
UNITS = (J // HALF) * N_TILES
GROUP = 16
RUN = 4
ALIGN = 64

HI_MASK = 0xFFF00000 - (1 << 32)
HI_MASK_PAIR = 0xFFF0FFF0 - (1 << 32)
SIGN_BIT = -(1 << 31)

WK0_PIECES = (slice(0, 128), slice(128, 256), slice(256, 512))
LEFT, RIGHT = slice(0, N // 2), slice(N // 2, N)
QUARTERS = (slice(0, HALF // 2), slice(HALF // 2, HALF))

KE_BANK = (0, 1, 2, 3, 0, 2, 4, 2)
VE_BANK = (4, 5, 6, 7, 1, 3, 5, 0)
ON_GPSIMD = (1, 3, 4, 5, 6)


def tile_list_hl_hway_kernel(tc, xT, wgt, wk, wv, bg, res, offs, out):
    nc = tc.nc
    with ExitStack() as ctx:
        keep = ctx.enter_context(tc.tile_pool(name="keep", bufs=1))
        ring = ctx.enter_context(tc.tile_pool(name="ring", bufs=2))
        mixes = ctx.enter_context(tc.tile_pool(name="mixes", bufs=4))
        psum = ctx.enter_context(tc.psum_pool(name="psum", bufs=1))

        def width(cols):
            return cols.stop - cols.start

        def n_tile(t):
            return slice(t * P, (t + 1) * P)

        def j_half(h):
            return slice(h * HALF, (h + 1) * HALF)

        def by_planes(ap):
            return ap.rearrange("p i (c u) -> p c i u", u=RUN)

        def as_packed(ap):
            return ap.rearrange("p (c u i) -> p c i u", u=RUN, i=PLANES)

        def codes_and_scales(name, columns):
            return (keep.tile([P, columns], U32, name=name + "_codes", align_bytes=ALIGN),
                    keep.tile([P, columns], U8, name=name + "_scales", align_bytes=ALIGN))

        def quantize(mx, cols, packed):
            codes, scales = mx
            nc.vector.quantize_mx(out=codes[:, cols].bitcast(FP8X4), scales=scales[:, cols], in_=packed[:])

        def bank(number, shape):
            return psum.tile(shape, F32, name="bank%d" % number)

        offs_sb = keep.tile([P, J // GROUP], U16, name="offs_sb")
        wgt_sb = [keep.tile([P, HALF], F32, name="wgt%d" % h, align_bytes=ALIGN) for h in range(J // HALF)]
        bg_sb = keep.tile([P, N_TILES], F32, name="bg_sb")
        planes = {(a, i): keep.tile([P, T], F32, name="plane%d%d" % (a, i)) for a in range(PASSES) for i in range(PLANES)}
        res_sb = [keep.tile([P, HALF], F32, name="res%d" % u, align_bytes=ALIGN) for u in range(UNITS)]
        w_mx = {(m, a): codes_and_scales("%s%d" % (m, a), N) for m in ("hi", "lo", "v") for a in range(PASSES)}
        x_mx = {(a, h): codes_and_scales("x%d%d" % (a, h), HALF) for a in range(PASSES) for h in range(J // HALF)}

        warm = keep.tile([P, 1], F32, name="warm")
        nc.vector.memset(warm[:], 0.0)
        nc.scalar.activation(out=warm[:], in_=warm[:], func=ACT.Sigmoid)

        def load_weight(name, w, a, cols):
            tile = keep.tile([P, PLANES, width(cols)], F32, name="%s%d_%d" % (name, a, cols.start))
            rows = w[a * K_PASS:(a + 1) * K_PASS, :].rearrange("(p i) n -> p i n", i=PLANES)
            nc.sync.dma_start(out=tile[:], in_=rows[:, :, cols])
            return tile

        def load_plane(a, i):
            rows = xT[a * K_PASS:(a + 1) * K_PASS, :].rearrange("(p i) t -> p i t", i=PLANES)
            nc.sync.dma_start(out=planes[a, i][:], in_=rows[:, i, :])

        wk0 = [load_weight("wk", wk, 0, cols) for cols in WK0_PIECES]
        nc.sync.dma_start(offs_sb[:], offs)
        nc.sync.dma_start(out=wgt_sb[0][:], in_=wgt[:, j_half(0)])
        load_plane(0, 0)
        wk1 = load_weight("wk", wk, 1, slice(0, N))
        nc.sync.dma_start(out=wgt_sb[1][:], in_=wgt[:, j_half(1)])
        for i in range(1, PLANES):
            load_plane(0, i)
        for i in range(PLANES - 1):
            load_plane(1, i)
        wv_left = [load_weight("wv", wv, a, LEFT) for a in range(PASSES)]
        load_plane(1, PLANES - 1)
        wv_right = [load_weight("wv", wv, a, RIGHT) for a in range(PASSES)]
        with nc.allow_non_contiguous_dma(reason="one bias value for each partition and n-tile"):
            nc.sync.dma_start(out=bg_sb[:], in_=bg.rearrange("(t p) -> p t", p=P))
        for u in range(UNITS):
            nc.sync.dma_start(out=res_sb[u][:], in_=res[n_tile(u % N_TILES), j_half(u // N_TILES)])

        hi0, lo0 = [], []

        def split_hi0(n):
            hi = keep.tile([P, width(WK0_PIECES[n]) * PLANES], BF16, name="hi0_%d" % n, align_bytes=ALIGN)
            nc.scalar.copy(out=as_packed(hi[:]), in_=by_planes(wk0[n][:].bitcast(BF16)[:, :, 1::2]))
            nc.vector.tensor_scalar(out=hi[:].bitcast(I32), in0=hi[:].bitcast(I32), scalar1=HI_MASK_PAIR, scalar2=None,
                                    op0=ALU.bitwise_and)
            hi0.append(hi)

        def split_lo0(n):
            lo = keep.tile([P, width(WK0_PIECES[n]) * PLANES], BF16, name="lo0_%d" % n, align_bytes=ALIGN)
            nc.vector.tensor_tensor(out=as_packed(lo[:]), in0=by_planes(wk0[n][:]), in1=as_packed(hi0[n][:]), op=ALU.subtract)
            lo0.append(lo)

        pieces = len(WK0_PIECES)
        for step in range(pieces + 2):
            if step < pieces:
                split_hi0(step)
            if 1 <= step <= pieces:
                split_lo0(step - 1)
                quantize(w_mx["hi", 0], WK0_PIECES[step - 1], hi0[step - 1])
            if step >= 2:
                quantize(w_mx["lo", 0], WK0_PIECES[step - 2], lo0[step - 2])

        neg_bg = keep.tile([P, N_TILES], F32, name="neg_bg")
        nc.scalar.activation(out=neg_bg[:], in_=bg_sb[:], func=ACT.Copy, scale=-1.0)

        identity = keep.tile([P, P], F32, name="identity")
        make_identity(nc, identity[:])

        neg_hi1 = keep.tile([P, PLANES, N], F32, name="neg_hi1")
        nc.vector.tensor_scalar(out=neg_hi1[:].bitcast(I32), in0=wk1[:].bitcast(I32), scalar1=HI_MASK, scalar2=SIGN_BIT,
                                op0=ALU.bitwise_and, op1=ALU.bitwise_xor)
        lo1 = keep.tile([P, N * PLANES], BF16, name="lo1", align_bytes=ALIGN)
        lo1_turned = []

        def turn_lo1(t):
            sums = bank(KE_BANK[t], [P, PLANES, P])
            for i in range(PLANES):
                nc.tensor.matmul(sums[:, i, :], lhsT=wk1[:, i, n_tile(t)], rhs=identity[:], start=True, stop=False,
                                 is_transpose=True)
                nc.tensor.matmul(sums[:, i, :], lhsT=neg_hi1[:, i, n_tile(t)], rhs=identity[:], start=False, stop=True,
                                 is_transpose=True)
            turned = ring.tile([P, PLANES * P], BF16, name="lo1_turned")
            nc.scalar.copy(out=turned[:].rearrange("n (u p e) -> n u p e", u=2, e=2),
                           in_=sums[:].rearrange("n (u e) p -> n u p e", u=2))
            lo1_turned.append(turned)

        def return_lo1(t):
            back = bank(VE_BANK[t], [P, 2, P])
            words = lo1_turned[t][:].bitcast(F32)
            for u in range(2):
                nc.tensor.transpose(back[:, u, :], words[:, n_tile(u)], identity[:])
            packed_words = lo1[:, t * P * PLANES:(t + 1) * P * PLANES].bitcast(F32)
            nc.scalar.copy(out=packed_words.rearrange("p (n u) -> p n u", u=2), in_=back[:].rearrange("p u n -> p n u"))

        for step in range(N_TILES + 1):
            if step < N_TILES:
                turn_lo1(step)
            if step >= 1:
                return_lo1(step - 1)
        hi1 = keep.tile([P, N * PLANES], BF16, name="hi1", align_bytes=ALIGN)
        nc.scalar.activation(out=as_packed(hi1[:]), in_=by_planes(neg_hi1[:]), func=ACT.Copy, scale=-1.0)

        def picks(pool, cols, tag):
            return pool.tile([P, PLANES, width(cols)], F32, name="picked", tag=tag, align_bytes=ALIGN)

        def gather(picked, a, i, h, cols):
            first = (h * HALF + cols.start) // GROUP
            nc.vector.tensor_tensor(out=picked[:, i, :],
                                    in0=planes[a, i][:].indirect(offs_sb[:, first:first + width(cols) // GROUP]),
                                    in1=wgt_sb[h][:, cols], op=ALU.mult)

        def pack(pool, source, name):
            packed = pool.tile([P, source.shape[2] * PLANES], BF16, name=name, align_bytes=ALIGN)
            nc.scalar.copy(out=as_packed(packed[:]), in_=by_planes(source[:]))
            return packed

        ke, ve = {}, {}

        def product(sums, m, a, u, start, stop):
            w_codes, w_scales = w_mx[m, a]
            x_codes, x_scales = x_mx[a, u // N_TILES]
            cols = n_tile(u % N_TILES)
            nc.tensor.matmul_mx(out=sums[:], lhsT=w_codes[:, cols].bitcast(FP8X4), lhsT_scale=w_scales[:, cols],
                                rhs=x_codes[:].bitcast(FP8X4), rhs_scale=x_scales[:], start=start, stop=stop)

        def ke_pass(a, u):
            if a == 0:
                ke[u] = bank(KE_BANK[u], [P, HALF])
            product(ke[u], "hi", a, u, a == 0, False)
            product(ke[u], "lo", a, u, False, a == PASSES - 1)

        def ve_pass(a, u):
            if a == 0:
                ve[u] = bank(VE_BANK[u], [P, HALF])
            product(ve[u], "v", a, u, a == 0, a == PASSES - 1)

        full = slice(0, HALF)
        picked0 = [picks(ring, full, "picked") for h in range(J // HALF)]
        for i in range(PLANES):
            for h in range(J // HALF):
                gather(picked0[h], 0, i, h, full)
        quantize(w_mx["hi", 1], slice(0, N), hi1)
        quantize(w_mx["lo", 1], slice(0, N), lo1)
        packed0 = [pack(ring, picked0[h], "packed_x") for h in range(J // HALF)]

        picked1 = picks(keep, full, "picked1")
        for h in range(J // HALF):
            gather(picked1, 1, h, 0, full)
            quantize(x_mx[0, h], full, packed0[h])
        packed_v = [pack(keep, wv_left[a], "packed_v_left%d" % a) for a in range(PASSES)]
        gather(picked1, 1, PLANES - 2, 0, full)
        for a in range(PASSES):
            quantize(w_mx["v", a], LEFT, packed_v[a])
        gather(picked1, 1, PLANES - 1, 0, full)
        packed1 = pack(ring, picked1, "packed_x")
        left_units = range(LEFT.stop // P)
        for u in range(N_TILES):
            ke_pass(0, u)
        for u in left_units:
            ve_pass(0, u)

        quarter0 = picks(keep, QUARTERS[0], "wgt0")
        for i in range(PLANES):
            gather(quarter0, 1, i, 1, QUARTERS[0])
        quantize(x_mx[1, 0], full, packed1)
        packed_v = [pack(keep, wv_right[a], "packed_v_right%d" % a) for a in range(PASSES)]
        packed_quarter0 = pack(ring, quarter0, "packed_x")
        quarter1 = picks(keep, QUARTERS[1], "picked1")
        for i in range(PLANES):
            gather(quarter1, 1, i, 1, QUARTERS[1])
        for a in range(PASSES):
            quantize(w_mx["v", a], RIGHT, packed_v[a])
        packed_quarter1 = pack(ring, quarter1, "packed_x")
        quantize(x_mx[1, 1], QUARTERS[0], packed_quarter0)
        quantize(x_mx[1, 1], QUARTERS[1], packed_quarter1)

        carry, mix = {}, {}

        def unit_tile(name, slot):
            return keep.tile([P, HALF], F32, name=name, tag=slot, align_bytes=ALIGN)

        def make_carry(u):
            t = u % N_TILES
            carry[u] = unit_tile("carry", "carry%d" % u)
            nc.scalar.activation(out=carry[u][:], in_=ke[u][:], func=ACT.Sigmoid, bias=neg_bg[:, t:t + 1], scale=-1.0)

        def difference(u, slot=None):
            mix[u] = unit_tile("mix", slot) if slot else mixes.tile([P, HALF], F32, name="mix")
            nc.vector.tensor_tensor(out=mix[u][:], in0=ve[u][:], in1=res_sb[u][:], op=ALU.subtract)

        def weigh(u):
            engine = nc.gpsimd if u in ON_GPSIMD else nc.vector
            engine.tensor_tensor(out=mix[u][:], in0=mix[u][:], in1=carry[u][:], op=ALU.mult)

        def finish(u, slot=None):
            result = unit_tile("result", slot) if slot else mix[u]
            nc.vector.tensor_tensor(out=result[:], in0=ve[u][:], in1=mix[u][:], op=ALU.subtract)
            nc.sync.dma_start(out=out[n_tile(u % N_TILES), j_half(u // N_TILES)], in_=result[:])

        for u in range(N_TILES):
            ke_pass(1, u)
            if u not in left_units:
                ve_pass(0, u)
            ve_pass(1, u)
            make_carry(u)

        difference(0)
        difference(1)
        weigh(0)
        weigh(1)
        difference(2, "carry0")
        finish(0)
        difference(3, "res2")
        weigh(2)
        weigh(3)
        finish(1)

        last = UNITS - 1
        for u in range(N_TILES, UNITS):
            if u == last:
                for a in range(PASSES):
                    ve_pass(a, u)
            for a in range(PASSES):
                ke_pass(a, u)
            make_carry(u)
            if u != last:
                for a in range(PASSES):
                    ve_pass(a, u)
            difference(u)
            finish(u - 2, "res%d" % u)
            weigh(u)
        finish(last - 1, "carry%d" % last)
        finish(last)
